import numpy as np, ml_dtypes
CORES = [40,41,42,43,44,45,46,47]
N = 8
import mx_ref
BF = ml_dtypes.bfloat16
def gcols(t, e):
    v = np.concatenate([t.reshape(8, 16, -1, 4), np.zeros((8, 16, 1, 4), BF)], axis=2)
    return np.ascontiguousarray(np.stack([v[g][:, e[g]] for g in range(8)])).reshape(128, -1)
def tile(rs):
    return np.stack(rs, axis=2).reshape(128, -1).astype(BF)
def pick(q, e):
    c = np.concatenate([q[0].reshape(128, -1, 4), np.zeros((128, 1, 4), np.uint8)], axis=1); s = np.concatenate([q[1], np.ones((16, 1), np.uint8)], axis=1)
    return (np.ascontiguousarray(c[:, e].reshape(128, -1)), np.ascontiguousarray(s[:, e]))
def join(*qs):
    return (np.concatenate([q[0] for q in qs], axis=1), np.concatenate([q[1] for q in qs], axis=1))
def put(q, e, v):
    c, s = q[0].reshape(128, -1, 4).copy(), q[1].copy(); c[:, e] = v[0].reshape(128, -1, 4); s[:, e] = v[1]
    return (c.reshape(128, -1), s)
def pk(c, s):
    return (np.ascontiguousarray(c), mx_ref.live(s))
def emit(q):
    return q[0], q[1]
def packed(v, rng):
    q = [mx_ref.quantize(np.ascontiguousarray(v[r])) for r in range(N)]
    return np.stack([a for a, b in q]), np.stack([mx_ref.plane(b, rng) for a, b in q])
def f(rng, *shape):
    return mx_ref.flush((rng.standard_normal(shape, dtype=np.float32) * np.exp2(rng.integers(-2, 3, shape[:-1] + (1,)))).astype(BF))
def wide(rng, *shape, cols=0):
    v = rng.standard_normal(shape, dtype=np.float32) * np.exp2(rng.integers(-12, 13, shape)).astype(np.float32)
    if cols: v *= np.repeat(np.exp2(rng.integers(-cols, cols + 1, shape[:-2] + (1, shape[-1] // 4))) * (rng.random(shape[:-2] + (1, shape[-1] // 4)) > 0.0625), 4, axis=-1).astype(np.float32)
    return mx_ref.flush(v.astype(BF))
C, A, R = 256, 128, 3
STEP = [1, 2, 4]
def places(p):
    return np.argsort(np.argsort(-(p[::16] + np.float32(0.0)), axis=1, kind="stable"), axis=1)
def neighbours(a, b):
    below = (a[:, None] < a[:, :, None]) & (b[:, None] < b[:, :, None])
    above = below.transpose(0, 2, 1)
    def best(m, k):
        return np.where(m.any(axis=2), np.argmax(np.where(m, k[:, None], -1), axis=2), np.arange(C))
    return best(below, a), best(below, b), best(above, C - a), best(above, C - b), np.sum(below, axis=2) % 2
def parts(m):
    return np.repeat(np.repeat(m, 16, axis=0), 4, axis=1)
def toggle(t, la, lb, ua, ub, m):
    low = np.maximum(gcols(t, la).astype(np.float32), gcols(t, lb).astype(np.float32))
    high = np.minimum(gcols(t, ua).astype(np.float32), gcols(t, ub).astype(np.float32))
    v = (low + high).astype(BF)
    h = (v.astype(np.float32) - t.astype(np.float32)).astype(BF)
    new, k = t.copy(), parts(m)
    new[k] = h[k]
    return new
def gput(t, e, h):
    a, b = t.reshape(8, 16, -1, 4).copy(), h.reshape(8, 16, -1, 4)
    for g in range(8): a[g][:, e[g]] = b[g]
    return a.reshape(128, -1)
def big(v):
    v = v.astype(np.float32)
    v[np.abs(v) < np.float32(2.0 ** -16)] = 0
    return v.astype(BF)
def numbers_of(rng):
    return {"x": big(f(rng, N, 128, 4 * C)), "u": np.array(f(rng, N, 128, 512)), "v": np.array(f(rng, N, 128, 512))}
def weights(rng, still=[]):
    w = np.array(f(rng, N, 128, 2048)).reshape(N, 8, 16, 4, 8, 16, 4)
    for i in still:
        w[:, :, i] = 0
        w[:, :, :, :, :, i] = 0
    c, p = packed(w.reshape(N, 128, 2048), rng)
    return {"wc": c, "ws": p}
def signs(rng):
    return np.stack([rng.permutation(8) % 2 * 2.0 - 1.0 for r in range(N)])
def digits(k, n):
    return ((k[..., None] >> np.arange(n)) & 1) * np.exp2(np.arange(n) * 1.0)
def setup_inputs(rng):
    return {**numbers_of(rng), **weights(rng)}
def setup_inputs_ties(rng):
    d = numbers_of(rng)
    e = rng.permutation(N)
    x = d["x"].reshape(N, 8, 16, C, 4)
    for r in range(N):
        k = np.zeros(C, int) if r == e[0] else rng.permutation(C) % 3
        a = x[r][:, :8, :3].copy()
        a[:, :, 2] = 0
        x[r][:, :8] = a[:, :, k]
    x[e[1]] = 0
    u = d["u"].reshape(N, 8, 16, 128, 4)
    u[:, :, 8:, ::16] = 0
    return {"x": x.reshape(N, 128, 4 * C), "u": u.reshape(N, 128, 512), "v": d["v"], **weights(rng, range(8))}
def setup_inputs_near(rng):
    d = numbers_of(rng)
    x = d["x"].astype(np.float32).reshape(N, 8, 16, C, 4)
    u = d["u"].reshape(N, 128, 128, 4)
    u[:, :, ::16] = 0
    o, c = rng.permutation(N) % 4, signs(rng)
    z = digits(np.argsort(rng.random((N, 8, C)), axis=2) // 2, 8)
    x[:, :, 0] = 0
    x[:, :, 8:] = 0
    for r in range(N):
        if o[r] < 2: x[r, :, 0, :, 0] = c[r][:, None]
        k = z[r] * 2.0 ** -23 if o[r] < 2 else z[r] * c[r][:, None, None] * 2.0 ** -30
        x[r, :, 8] = k[:, :, :4]
        x[r, :, 9] = k[:, :, 4:]
        size = 1.0 if o[r] == 0 else 2.0 ** -30
        for h in range(0, 128, 16):
            u[r, h, h, 0] = size
            u[r, h + 8:h + 10, h] = size
    return {"x": x.reshape(N, 128, 4 * C).astype(BF), "u": u.reshape(N, 128, 512), "v": d["v"], **weights(rng, [0, 8, 9, 10, 11, 12, 13, 14, 15])}
def setup_inputs_chains(rng):
    d = numbers_of(rng)
    x = d["x"].astype(np.float32).reshape(N, 8, 16, C, 4)
    u = d["u"].reshape(N, 128, 128, 4)
    h = C // 2
    o = np.argsort(rng.random((N, 8, C)), axis=2)
    for r in range(N):
        p = r ^ STEP[0]
        if r < p:
            k = rng.permutation(8)
            for g in range(8):
                a = o[r, g]
                if k[g] == 0: o[p, g] = a
                if k[g] == 1: o[p, g] = a[::-1]
                if k[g] == 2: o[p, g] = np.concatenate([a[:1], a[1:][::-1]])
                if k[g] == 3: o[p, g] = np.concatenate([a[:-1][::-1], a[-1:]])
                if k[g] == 4: o[p, g] = np.concatenate([a[h:], a[:h]])
                if k[g] == 5: o[p, g] = np.concatenate([a[:h][::-1], a[h:][::-1]])
                if k[g] == 6: o[p, g] = a.reshape(-1, 2)[:, ::-1].reshape(-1)
    z = digits(C - 1 - np.argsort(o, axis=2), 12)
    for i in range(3): x[:, :, 8 + i] = z[:, :, :, 4 * i:4 * i + 4]
    k = np.where(rng.permutation(N) < N // 2, 2.0 ** -30, 1.0).astype(np.float32).astype(BF)
    u[:, :, ::16] = 0
    for i in range(0, 128, 16): u[:, i + 8:i + 11, i] = k[:, None, None]
    return {"x": x.reshape(N, 128, 4 * C).astype(BF), "u": u.reshape(N, 128, 512), "v": d["v"], **weights(rng, [8, 9, 10])}
def setup_inputs_huge(rng):
    d = numbers_of(rng)
    mixed = rng.permutation(8) < 4
    side = np.array([1.0 - 2.0 * (bin(r).count("1") % 2) for r in range(N)])
    c = rng.permutation(C) % 2 * 2.0 - 1.0
    k = np.where(mixed[:, None], np.argsort(rng.random((8, C)), axis=1), rng.integers(0, 32, (N, 8, C)))
    z = digits(k, 12) * np.where(mixed, 2.0 ** 21, 2.0 ** 18)[:, None, None]
    p = np.ones(8)
    p[~mixed] = rng.permutation(4) % 2 * 2.0 - 1.0
    s = np.where(mixed, side[:, None], p)
    x = np.zeros((N, 8, 16, C, 4))
    x[:, :, :8] = (s[:, :, None] * np.where(mixed[:, None], c, 1.0))[:, :, None, :, None] * 2.0 ** 30
    for i in range(3): x[:, :, 8 + i] = z[:, :, :, 4 * i:4 * i + 4] * s[:, :, None, None]
    x[:, :, 11:] = 2.0 ** 20 * (0.5 + 0.5 * rng.random((N, 8, 5, C, 4))) * rng.choice([-1.0, 1.0], (N, 8, 5, C, 4))
    u = d["u"].reshape(N, 8, 16, 128, 4)
    u[:, :, :, ::16] = 0
    w = 2.0 ** 30 * (1 - 0.125 * rng.random((8, 8, 4))) * p[:, None, None]
    q = np.ones((N, 8))
    for r in range(N): q[r, ~mixed] = rng.permutation(4) % 2 * 2.0 - 1.0
    for g in range(8):
        for h in range(8):
            if mixed[h] == mixed[g]: u[:, h, :8, 16 * g] = (q[:, g][:, None, None] * w[h]).astype(np.float32).astype(BF)
        u[:, g, 8:11, 16 * g] = 2.0 ** 30
    return {"x": x.astype(np.float32).reshape(N, 128, 4 * C).astype(BF), "u": u.reshape(N, 128, 512), "v": d["v"], **weights(rng, range(11))}
def setup_inputs_spread(rng):
    d = setup_inputs(rng)
    d["x"] = big(wide(rng, N, 128, 4 * C, cols=6))
    return d
def check_inputs(d):
    b = []
    for k in ("x", "u", "v"):
        a = np.abs(d[k].astype(np.float32))
        if not (np.isfinite(a).all() and ((a == 0) | (a >= 2.0 ** -30) & (a <= 2.0 ** 30)).all()): b.append("a value of " + k)
    if ((d["wc"] & 0x7F) == 0x7F).any(): b.append("a code of wc that is no number")
    z = np.zeros((128, 4, 4), np.float32)
    z[:, 1] = 2.0 ** -30
    z[:, 2] = 2.0 ** 30
    c, s = emit(mx_ref.quantize(z.reshape(128, 16).astype(BF)))
    for r in range(N):
        p = mx_ref.live(d["ws"][r])
        if not ((p == s[0, 0]) | (p >= s[0, 1]) & (p <= s[0, 2])).all(): b.append("a scale of ws")
    return b
def reference(x, u, v, wc, ws):
    qu = [mx_ref.quantize(u[r]) for r in range(N)]
    lay = [pk(wc[r], ws[r]) for r in range(N)]
    now = [x[r] for r in range(N)]
    for t in range(R):
        a = [places(mx_ref.matmul(qu[r], mx_ref.quantize(now[r]))) for r in range(N)]
        e, own, sent = [], [], []
        for r in range(N):
            b = a[r ^ STEP[t]]
            la, lb, ua, ub, odd = neighbours(a[r], b)
            for k in range(2): now[r] = toggle(now[r], la, lb, ua, ub, odd == k)
            e.append(np.argsort(-(a[r] + b), axis=1, kind="stable")[:, :A])
            own.append(gcols(now[r], e[r]))
            sent.append(mx_ref.quantize(own[r]))
        for r in range(N):
            q = sent[r ^ STEP[t]]
            h = tile([mx_ref.matmul(pick(lay[r], np.arange(128 * i, 128 * i + 128)), q) * np.float32(0.015625) + own[r][:, i::4].astype(np.float32) for i in range(4)])
            now[r] = gput(now[r], e[r], h)
    y = np.zeros((N, 128, C), np.float32)
    oc, osc = np.zeros((N, 128, 4 * C), np.uint8), np.zeros((N, 16, C), np.uint8)
    for r in range(N):
        q = mx_ref.quantize(now[r])
        y[r] = mx_ref.matmul(mx_ref.quantize(v[r]), q)
        oc[r], osc[r] = emit(q)
    return {"y": y, "oc": oc, "osc": osc}

from concourse.mybir import dt, AluOpType as A, ActivationFunctionType as F

C = 256
R = 3
STEP = [1, 2, 4]
BIG = 1.0e25
NV = 9
EARLY = 4
SM = 9
EA = 4
CODE = "float8_e4m3fn_x4"

SCRATCH = {
    "pSV": ("psum", [128, 512], "float32"), "pSS": ("psum", [128, 512], "float32"),
    "pR": ("psum", [128, 2048], "float32"), "pY": ("psum", [128, 512], "float32"),
}


def _sb(names, shape, dtype):
    for n in names.split():
        SCRATCH[n] = ("sbuf", shape, dtype)


_sb("x0 X lw hi Vt", [128, 1024], "bfloat16")
_sb("ub vb Ft", [128, 512], "bfloat16")
_sb("uq uq2 vq fq0 fq1 fq2 lq0 lq1 lq2", [128, 128], CODE)
_sb("us us2 vs fs0 fs1 fs2 ls0 ls1 ls2", [128, 128], "uint8")
_sb("wq", [128, 512], CODE)
_sb("wp", [128, 512], "uint8")
_sb("xq0 xq1 xq2 xq3", [128, 256], CODE)
_sb("xs0 xs1 xs2 xs3", [128, 256], "uint8")
_sb("aw0 aw1 aw2 bw0 bw1 bw2 colw rep zw erw0 erw1 erw2 finw upick fw", [128, 16], "uint16")
_sb("lo0 lo1 lo2 lp0 lp1 lp2 offs", [128, 32], "uint16")
_sb("ci", [128, 48], "int32")
_sb("i16 K dl ndl tge tle iob dn dp ne colb brow prow pm ps dm ds", [128, 256], "bfloat16")
_sb("mmin rst iof t256 tmp hold akr keyr vrow frow", [128, 256], "float32")
_sb("ptab", [128, 288], "float32")
_sb("qc kw inF inB cst Ga Lb E2 xg akw keyw npi Ac za sg er f1", [128, 16], "float32")
_sb("PM", [128, 16, 256], "bfloat16")
_sb("PO", [128, 16, 128], "bfloat16")
_sb("FW BW", [128, 16, 272], "bfloat16")
_sb("FO BO", [128, 16, 272], "float16")
_sb("tab rr Rs", [128, 512], "float32")
_sb("rm rs", [128, 2, 256], "float16")
_sb("vm vsc", [128, 256], "float16")
_sb("ej", [128, 2, 256], "bfloat16")
_sb("W0 W1 W2 W3", [128, 640], "bfloat16")
_sb("G1 G2", [128, 2048], "bfloat16")

DMAS = ["x", "u", "v", "wc", "ws", "y", "oc", "s0", "s1", "s2", "s3"]
SEMAPHORES = ["cV", "cS", "cP", "cG", "sent"] + ["d_" + n for n in DMAS] + \
    ["%s%d" % (k, t) for k in ("ra", "rl", "ru", "re", "rf") for t in range(R)]


def _emit(g, T, ops):
    queue = {"V": g.vector, "S": g.scalar, "P": g.tensor, "G": g, "Y": g.sync}
    seq, clock, done = {}, {q: {} for q in queue}, []
    writer, readers, waits = {}, {}, []
    for n, o in enumerate(ops):
        q = o["q"]
        deps = set()
        for k in o["r"] + o["w"]:
            if k in writer:
                deps.add(writer[k])
        for k in o["w"]:
            deps.update(readers.get(k, []))
        mine = []
        for d in sorted(deps, reverse=True):
            key, num = ops[d]["at"]
            if clock[q].get(key, 0) < num:
                mine.append(d)
                ops[d]["need"] = True
                for kk, vv in done[d].items():
                    clock[q][kk] = max(clock[q].get(kk, 0), vv)
        arr = []
        for s, v in o["arr"]:
            if clock[q].get("@" + s, 0) < v:
                arr.append((s, v))
                clock[q]["@" + s] = v
        waits.append((mine, arr))
        key = o["dma"] or q
        seq[key] = seq.get(key, 0) + 1
        o["at"] = (key, seq[key])
        c = dict(clock[q])
        c[key] = seq[key]
        done.append(c)
        for k in o["w"]:
            writer[k] = n
            readers[k] = []
        for k in o["r"]:
            if o["w"] or o["dma"]:
                readers.setdefault(k, []).append(n)
    count = {}
    for n, o in enumerate(ops):
        e = queue[o["q"]]
        for d in waits[n][0]:
            e.wait_ge(T.sem[ops[d]["sem"][0]], ops[d]["sem"][1])
        for s, v in waits[n][1]:
            e.wait_ge(T.sem[s], v)
        ins = o["fn"]()
        if o["dma"]:
            o["sem"] = (o["dma"], 16)
            count[o["dma"]] = 16
            ins.then_inc(T.sem[o["dma"]], 16)
        elif o["need"]:
            s = "c" + o["q"]
            count[s] = count.get(s, 0) + 1
            o["sem"] = (s, count[s])
            ins.then_inc(T.sem[s], 1)
    for s in count:
        g.wait_ge(T.sem[s], count[s])


def rank_program(g, core, T, topo):
    rank = T.rank_of(core)
    if rank is None:
        return
    V, S, P = g.vector, g.scalar, g.tensor
    ops, sent = [], [0]

    def op(q, fn, r, w, arr=(), dma=None):
        ops.append({"q": q, "fn": fn, "r": r.split(), "w": w.split(), "arr": list(arr), "dma": dma, "need": False})

    def tt(out, a, b, o, r, w, arr=()):
        op("V", lambda: V.tensor_tensor(out, a, b, o), r, w, arr)

    def ts(out, a, s1, o1, r, w, s2=None, o2=None, arr=()):
        if o2 is None:
            op("V", lambda: V.tensor_scalar(out, a, s1, None, o1), r, w, arr)
        else:
            op("V", lambda: V.tensor_scalar(out, a, s1, s2, o1, o2), r, w, arr)

    def cp(out, a, r, w, arr=()):
        op("V", lambda: V.tensor_copy(out, a), r, w, arr)

    def fill(out, c, w):
        op("V", lambda: V.memset(out, c), "", w)

    def scan(out, d0, d1, ini, o0, o1, r, w):
        op("V", lambda: V.tensor_tensor_scan(out, d0, d1, ini, o0, o1), r, w)

    def act(out, a, f, r, w, arr=(), **kw):
        op("S", lambda: S.activation(out, a, f, **kw), r, w, arr)

    def iota(out, pat, base, cm, w):
        op("G", lambda: g.iota(out, pat, base, cm, allow_small_or_imprecise_dtypes=True), "", w)

    def quant(q, s, a, r, w):
        op("V", lambda: V.quantize_mx(q, s, a), r, w)

    def mm(out, lq, ls, rq, rs, r, w, arr=()):
        op("P", lambda: P.matmul_mx(out, lq, ls, rq, rs, True, True), r, w, arr)

    def dma(q, name, out, a, r, w):
        e = g.sync if q == "Y" else g.scalar
        op(q, lambda: e.dma_start(out, a), r, w, dma="d_" + name)

    def send(peer, out, a, sem, r):
        rid, pid, ring = topo.addr(peer)
        m = topo.mask(core, peer)
        sent[0] += len(topo.engines(core, peer))
        op("G", lambda: g.remote_dma(out, a, T.sem[sem], T.sem.sent, pid, rid, m), r, "")

    def u8(v):
        return v.bitcast(dt.uint8)

    def rev(a, b):
        return slice(b - 1, a - 1 if a > 0 else None, -1)

    def each(form, js):
        return " ".join(form % j for j in js)

    def part(buf, b):
        return buf[:, b * C:b * C + C]

    ends = slice(15, None, 16)
    back = rev(0, C)
    W = [T.W0, T.W1, T.W2, T.W3]
    XA = "X0 X1 X2 X3"

    dma("Y", "x", T.x0[:], T.x[:], "", XA)
    dma("S", "u", T.ub[:], T.u[:], "", "ub")
    dma("Y", "wc", u8(T.wq[:]), T.wc[:], "", "wq")
    dma("S", "ws", T.wp[:], T.ws[:], "", "wp")
    dma("Y", "v", T.vb[:], T.v[:], "", "vb")
    iota(T.ci[:, 0:16], [[16, 16]], 0, 0, "ci0")
    iota(T.ci[:, 16:17], [[1, 1]], 0, 1, "ci1")
    iota(T.i16[:], [[0, 16], [1, 16]], 0, 0, "i16")
    iota(T.iof[:], [[1, C]], 0, 0, "iof")
    iota(T.ptab[:], [[0, 144], [-256, 2]], 256, 0, "ptab")
    q = T.qc[:, 0:1]
    fill(T.rst[:], BIG, "rst")
    cp(T.upick[:], T.ci[:, 0:16], "ci0", "upick")
    ts(T.ci[:, 32:33], T.ci[:, 16:17], 15, A.bitwise_and, "ci1", "ci2")
    fill(T.rst[:, 0::16], -BIG, "rst")
    cp(q, T.ci[:, 32:33], "ci2", "qc")
    fill(T.Ga[:], 0.0, "Ga")
    fill(T.Ac[:], 0.0, "Ac")
    ts(T.dl[:], T.i16[:], q, A.is_equal, "i16 qc", "dl")
    ts(T.cst[:], T.ci[:, 0:16], 16.0, A.add, "ci0", "cst")
    ts(T.kw[:], T.ci[:, 0:16], q, A.add, "ci0 qc", "kw")
    ts(T.rep[:], T.ci[:, 0:16], 15.0, A.add, "ci0", "rep")
    ts(T.tge[:], T.i16[:], q, A.is_ge, "i16 qc", "tge")
    ts(T.tle[:], T.i16[:], q, A.is_le, "i16 qc", "tle")
    ts(T.qc[:, 8:9], q, 128.0, A.add, "qc", "qc2")
    ts(T.inF[:], T.kw[:], 512.0, A.subtract, "kw", "inF")
    ts(T.inB[:], T.kw[:], 257.0, A.add, "kw", "inB")
    act(T.K[:], T.i16[:], F.Sign, "i16", "K")
    act(T.mmin[:], T.dl[:], F.Identity, "dl", "mmin", scale=2 * BIG, bias=-BIG)
    act(T.iob[:], T.iof[:], F.Copy, "iof", "iob")
    act(T.t256[:], T.iof[:], F.Copy, "iof", "t256", scale=256.0)
    act(T.dn[:], T.iof[:], F.Identity, "iof", "dn", bias=-256.0)
    act(T.dp[:], T.iof[:], F.Identity, "iof", "dp", bias=1.0)
    act(T.ndl[:], T.dl[:], F.Identity, "dl", "ndl", scale=-1.0, bias=1.0)
    quant(T.uq[:], T.us[:], T.ub[:], "ub", "uq")
    cp(T.uq2[:].bitcast(dt.uint32), T.uq[:].bitcast(dt.uint32).indirect(T.upick[:, 0:8]), "uq upick", "uq2")
    cp(T.us2[:], T.us[:].indirect(T.upick[:, 0:8]), "uq upick", "us2")

    for t in range(R):
        peer = T.cores[rank ^ STEP[t]]
        ne = len(topo.engines(peer, core))
        X = T.x0 if t == 0 else T.X
        xq, xs = T["xq%d" % t], T["xs%d" % t]
        aw, bw, lo, lp, erw = [T["%s%d" % (k, t)] for k in ("aw", "bw", "lo", "lp", "erw")]
        ab = [("ra%d" % t, ne * (2 if t == 0 else 1))]
        al, au, ae, af = [("rl%d" % t, ne)], [("ru%d" % t, ne)], [("re%d" % t, ne)], [("rf%d" % t, 2 * ne)]

        def planes(half):
            for b in range(4):
                op("G", lambda b=b, X=X: g.affine_select(part(W[b], half), X[:, b::4], [[1, C]], A.is_ge, 0.0, 0, 0),
                   "X%d" % b, "W%d%d" % (b, half))

        quant(xq[:], xs[:], X[:], XA, "xq")
        mm(T.pSV[:, 0:C], T.uq2[:], T.us2[:], xq[:], xs[:], "uq2 us2 xq", "pSV")
        mm(T.pSS[:, 0:C], T.uq2[:], T.us2[:], xq[:], xs[:], "uq2 us2 xq", "pSS")
        planes(0)
        tt(T.tmp[:], T.pSV[:, 0:C], T.mmin[:], A.min, "pSV mmin", "tmp")
        scan(T.hold[:], T.rst[:], T.tmp[:], -BIG, A.min, A.max, "rst tmp", "hold")

        def own(j):
            return T.hold[:, 16 * j + 15:16 * j + 16]

        def vmask(j):
            n = 16 * j + 16
            ts(T.PM[:, j, 0:n], T.pSV[:, 0:n], own(j), A.is_ge, "pSV hold", "PMa%d" % j)
            ts(T.PM[:, j, n:C], T.pSV[:, n:C], own(j), A.is_gt, "pSV hold", "PMb%d" % j)

        def vcount(j):
            scan(T.PO[:, j, :], T.PM[:, j, 0:128], T.PM[:, j, 128:C], T.ne[:, 16 * j + 15:16 * j + 16], A.add, A.add,
                 "PMa%d PMb%d ne" % (j, j), "PO%d" % j)

        def ssign(j):
            act(T.PM[:, j, :], T.pSS[:, 0:C], F.Sign, "pSS hold", "PMa%d PMb%d" % (j, j), bias=own(j), scale=-1.0)

        def scount(j):
            n = 16 * j + 16
            act(T.PM[:, j, 0:n], T.PM[:, j, 0:n], F.Relu, "PMa%d" % j, "PMa%d Lb%d" % (j, j), accum_out=T.Lb[:, j:j + 1])
            if n < C:
                act(T.PM[:, j, n:C], T.PM[:, j, n:C], F.Relu, "PMb%d Ga" % j, "PMb%d Ga%d" % (j, j), scale=-1.0, accum_out=T.Ga[:, j:j + 1])

        ssign(NV)
        for j in range(NV, 16):
            if j + 1 < 16:
                ssign(j + 1)
            scount(j)
        tt(T.dm[:], T.pSV[:, 0:C], T.hold[:], A.is_equal, "pSV hold", "dm")
        vmask(0)
        scan(T.ne[:], T.K[:], T.dm[:], 0.0, A.mult, A.subtract, "K dm", "ne")
        for j in range(NV):
            if j + 1 < NV:
                vmask(j + 1)
            if j == 1:
                tt(T.E2[:, NV:], T.ne[:, 16 * NV + 15::16], T.cst[:, NV:], A.add, "ne cst", "E2")
            vcount(j)
            if t == 0 and j == EARLY:
                cp(aw[:, 0:EARLY], T.PO[:, 0:EARLY, 127], each("PO%d", range(EARLY)), "awa")
                send(peer, bw[:, 0:EARLY], aw[:, 0:EARLY], "ra0", "awa")
        tt(T.xg[:, NV:], T.Ga[:, NV:], T.Lb[:, NV:], A.subtract, each("Lb%d", range(NV, 16)) + " Ga " + each("Ga%d", range(NV, 15)), "xg")
        tt(T.PO[:, NV:, 127], T.xg[:, NV:], T.E2[:, NV:], A.add, "xg E2", "POs")
        e0 = EARLY if t == 0 else 0
        pos = each("PO%d", range(NV)) + " POs"
        cp(aw[:, e0:], T.PO[:, e0:, 127], pos, "aw" if t == 0 else "aw awa")
        send(peer, bw[:, e0:], aw[:, e0:], "ra%d" % t, "aw")
        e0 = 8 if rank & STEP[t] else 0
        planes(1)

        cp(T.colb[:].indirect(aw[:]), T.iob[:], "aw awa iob", "colb")
        ts(T.akw[:], T.PO[:, :, 127], 256.0, A.mult, pos, "akw")
        tt(T.pm[:], T.colb[:], T.dl[:], A.mult, "colb dl", "pm")
        tt(T.akw[:], T.akw[:], T.kw[:], A.subtract, "akw kw", "akw")
        scan(T.ds[:], T.K[:], T.pm[:], 0.0, A.mult, A.add, "K pm", "ds")
        cp(T.colw[:], T.ds[:, ends], "ds", "colw")
        tt(T.akr[:], T.t256[:].indirect(aw[:]), T.iof[:], A.subtract, "aw awa t256 iof", "akr")

        act(T.brow[:], T.iob[:].indirect(bw[:]), F.Copy, "iob", "brow", ab)
        act(T.prow[:], T.brow[:].indirect(T.colw[:]), F.Copy, "brow colw", "prow")
        ts(T.keyw[:], bw[:], 256.0, A.mult, "", "keyw", arr=ab)
        tt(T.keyw[:], T.keyw[:], T.akw[:], A.add, "keyw akw", "keyw")
        tt(T.pm[:], T.brow[:].indirect(T.colw[:]), T.dl[:], A.mult, "brow colw dl", "pm")
        scan(T.ps[:], T.K[:], T.pm[:], 0.0, A.mult, A.add, "K pm", "ps")
        ts(T.npi[:], T.ps[:, ends], -1.0, A.mult, "ps", "npi")
        for j in range(15, 0, -1):
            act(T.FW[:, j, C - 16 * j:C], T.prow[:, 0:16 * j], F.Sign, "prow npi Ac", "FW%d Ac%d" % (j, j),
                bias=T.npi[:, j:j + 1], accum_out=T.Ac[:, j:j + 1])
        tt(T.dm[:], T.ps[:].indirect(T.rep[:]), T.prow[:], A.is_lt, "ps rep prow", "dm")
        tt(T.keyr[:], T.t256[:].indirect(bw[:]), T.akr[:], A.add, "t256 akr", "keyr", ab)
        tt(T.FW[:, :, C:C + 16], T.dm[:], T.tge[:], A.max, "dm tge", "FWd")
        tt(T.BW[:, :, 0:16], T.dm[:], T.tle[:], A.is_le, "dm tle", "BWd")
        scan(T.ds[:, back], T.dm[:, back], T.ndl[:, back], 0.0, A.add, A.mult, "dm ndl", "ds")

        def fscan(j):
            scan(T.FO[:, j, C - 16 * j:C + 16], T.FW[:, j, C - 16 * j:C + 16], T.dn[:, 0:16 * j + 16], T.inF[:, j:j + 1],
                 A.mult, A.min, "FW%d FWd dn inF" % j, "FO%d" % j)

        def bscan(j):
            n = C - 16 * j
            scan(T.BO[:, j, rev(0, n)], T.BW[:, j, rev(0, n)], T.dp[:, rev(16 * j, C)], T.inB[:, j:j + 1],
                 A.mult, A.max, "BW%d BWd dp inB" % j, "BO%d" % j)

        def smask(j):
            act(T.BW[:, j, 16:C - 16 * j], T.prow[:, 16 * j + 16:C], F.Sign, "prow ps", "BW%d" % j,
                bias=T.ps[:, 16 * j + 15:16 * j + 16], scale=-1.0)

        def eplace(j):
            act(T.ej[:, j % 2, :], T.keyr[:], F.Sign, "keyr keyw", "ej%d sg%d" % (j % 2, j),
                bias=T.keyw[:, j:j + 1], scale=-1.0, accum_out=T.sg[:, j:j + 1])

        def near(b, h):
            act(part(T.G1, 2 * b + h), W[b][:, 0:2 * C].indirect(lo[:, 16 * h:16 * h + 16]), F.Copy,
                "W%d0 W%d1 lo%d" % (b, b, h), "Ga%d%d" % (b, h))

        def extract(h):
            tt(T.rm[:, h, :], part(T.rr, h).indirect(aw[:]), T.dl[:], A.mult, "rr%d aw awa dl" % h, "rm%d" % h)

        def finish(h):
            scan(T.rs[:, h, :], T.K[:], T.rm[:, h, :], 0.0, A.mult, A.add, "K rm%d" % h, "rs%d" % h)

        def post(h):
            cp(lo[:, 16 * h:16 * h + 16], T.rs[:, h, ends], "rs%d" % h, "lo%d" % h)
            send(peer, lp[:, 16 * h:16 * h + 16], lo[:, 16 * h:16 * h + 16], "r%s%d" % ("lu"[h], t), "lo%d" % h)

        for j in range(SM):
            smask(j)
        fscan(0)
        bscan(15)
        for j in range(15, 0, -1):
            fscan(j)
        ts(T.za[:], T.Ac[:], 0.5, A.mult, "qc2 Ac " + each("Ac%d", range(1, 16)), "za", T.qc[:, 8:9], A.add)
        ts(T.offs[:, 0:16], T.FO[:, :, C + 15], 512.0, A.add, each("FO%d", range(16)), "offF")
        tt(T.za[:], T.za[:], T.ds[:, 0::16], A.add, "za ds", "za")
        bscan(0)
        cp(T.zw[:], T.za[:], "za", "zw")
        bscan(1)
        tt(T.tab[:, 0:C], T.ptab[:].indirect(T.zw[:]), T.colb[:], A.add, "ptab zw colb", "tabA")
        act(T.tab[:, C:], T.tab[:, 0:C], F.Copy, "tabA", "tabB")
        act(T.rr[:, 0:C], T.tab[:].indirect(T.offs[:, 0:16]), F.Copy, "tabA tabB offF", "rr0")
        for j in range(SM, 15):
            smask(j)
        for j in range(2, SM):
            bscan(j)
        extract(0)
        bscan(SM)
        finish(0)
        bscan(SM + 1)
        post(0)
        for j in range(EA):
            eplace(e0 + j)
        for j in range(SM + 2, 15):
            bscan(j)
        ts(T.offs[:, 16:32], T.BO[:, :, 0], 1.0, A.subtract, each("BO%d", range(16)), "offB")
        cp(T.rr[:, C:], T.tab[:].indirect(T.offs[:, 16:32]), "tabA tabB offB", "rr1")
        for b in range(4):
            near(b, 0)
        extract(1)
        finish(1)
        post(1)
        for b in range(4):
            near(b, 1)
        for j in range(EA, 8):
            eplace(e0 + j)
        act(T.vrow[:], T.tab[:, 0:C].indirect(aw[:]), F.Copy, "tabA aw awa", "vrow")

        def mx(G, name, b):
            tt(part(T.lw, b), W[b][:, 0:2 * C].indirect(lp[:, 0:16]), part(G, 2 * b), A.max, "W%d0 W%d1 %s%d0" % (b, b, name, b), "lw%d" % b, al)

        def mn(G, name, b):
            tt(part(T.hi, b), W[b][:, 0:2 * C].indirect(lp[:, 16:32]), part(G, 2 * b + 1), A.min, "W%d0 W%d1 %s%d1" % (b, b, name, b), "hi%d" % b, au)

        def add(b):
            tt(part(T.Vt, b), part(T.lw, b), part(T.hi, b), A.add, "lw%d hi%d" % (b, b), "Vt%d" % b)

        def sub(b, half):
            tt(part(W[b], half), part(T.Vt, b), part(W[b], 0), A.subtract, "Vt%d W%d0" % (b, b), "W%d%d" % (b, half))

        def far(b):
            act(T.G1[:, 2 * b * C:2 * (b + 1) * C], W[b][:, 0:2 * C].indirect(lp[:]), F.Copy, "W%d0 W%d1" % (b, b), "Ga%d0 Ga%d1" % (b, b), al + au)

        def mx2(b):
            tt(part(T.lw, b), part(T.G1, 2 * b), part(T.G2, 2 * b), A.max, "Ga%d0 Gb%d0" % (b, b), "lw%d" % b)

        def mn2(b):
            tt(part(T.hi, b), part(T.G1, 2 * b + 1), part(T.G2, 2 * b + 1), A.min, "Ga%d1 Gb%d1" % (b, b), "hi%d" % b)

        def both(b):
            act(T.G2[:, 2 * b * C:2 * (b + 1) * C], W[b][:, 0:2 * C].indirect(lo[:]), F.Copy, "W%d0 W%d1 lo0 lo1" % (b, b), "Gb%d0 Gb%d1" % (b, b))

        def pickf(b):
            act(T.Ft[:, b::4], W[b][:, 0:2 * C].indirect(T.fw[:, 0:8]), F.Copy, "W%d0 W%d1 fw" % (b, b), "F%d" % b)

        for b in range(4):
            mx(T.G1, "Ga", b)
        for b in range(4):
            mn(T.G1, "Ga", b)
            if b > 0:
                sub(b - 1, 1)
                both(b - 1)
            add(b)
            if b == 2:
                ts(erw[:, e0:e0 + 8], T.sg[:, e0:e0 + 8], -0.5, A.mult, each("sg%d", range(e0, e0 + 8)), "erw", 127.5, A.add)
                send(peer, erw[:, e0:e0 + 8], erw[:, e0:e0 + 8], "re%d" % t, "erw")
        mx(T.G2, "Gb", 0)
        sub(3, 1)
        far(2)
        both(3)
        far(3)
        mn(T.G2, "Gb", 0)
        mx(T.G2, "Gb", 1)
        add(0)
        cp(T.frow[:].indirect(erw[:]), T.vrow[:], "erw vrow", "frow", ae)
        sub(0, 0)
        tt(T.vm[:, 0:128], T.frow[:, 0:128], T.dl[:, 0:128], A.mult, "frow dl", "vm")
        mn(T.G2, "Gb", 1)
        scan(T.vsc[:, 0:128], T.K[:, 0:128], T.vm[:, 0:128], 0.0, A.mult, A.add, "K vm", "vsc")
        mx2(2)
        cp(T.fw[:, 0:8], T.vsc[:, 15:128:16], "vsc", "fw")
        pickf(0)
        add(1)
        mn2(2)
        sub(1, 0)
        pickf(1)
        mx2(3)
        mn2(3)
        add(2)
        add(3)
        sub(2, 0)
        pickf(2)
        sub(3, 0)
        cp(T.Ft[:, 3::4], W[3][:, 0:2 * C].indirect(T.fw[:, 0:8]), "W30 W31 fw", "F3")

        fq, fs, lq, ls = [T["%s%d" % (k, t)] for k in ("fq", "fs", "lq", "ls")]
        quant(fq[:], fs[:], T.Ft[:], "F0 F1 F2 F3", "fq")
        send(peer, u8(lq[:]), u8(fq[:]), "rf%d" % t, "fq")
        send(peer, ls[:], fs[:], "rf%d" % t, "fq")
        tt(T.vm[:], T.vrow[:], T.dl[:], A.mult, "vrow dl", "vm")
        ts(T.er[:], erw[:], 512.0, A.add, "erw", "er")
        scan(T.vsc[:], T.K[:], T.vm[:], 0.0, A.mult, A.add, "K vm", "vsc")
        ts(T.xg[:], T.er[:], 640.0, A.is_lt, "er", "xg")
        tt(T.f1[:], T.er[:], T.vsc[:, ends], A.subtract, "er vsc", "f1")
        tt(T.f1[:], T.f1[:], T.xg[:], A.mult, "f1 xg", "f1")
        tt(T.f1[:], T.f1[:], T.vsc[:, ends], A.add, "f1 vsc", "f1")
        cp(T.finw[:], T.f1[:], "f1", "finw")
        if t == 0:
            quant(T.vq[:], T.vs[:], T.vb[:], "vb", "vq")
        for b in range(4):
            mm(T.pR[:, 512 * b:512 * b + 128], T.wq[:, 128 * b:128 * b + 128], T.wp[:, 128 * b:128 * b + 128], lq[:], ls[:],
               "wq wp", "pR%d" % b, af)
        for b in range(4):
            act(T.Rs[:, 128 * b:128 * b + 128], T.pR[:, 512 * b:512 * b + 128], F.Copy, "pR%d" % b, "Rs%d" % b, scale=0.015625)
        for b in range(4):
            tt(W[b][:, 2 * C:], T.Rs[:, 128 * b:128 * b + 128], T.Ft[:, b::4], A.add, "Rs%d F%d" % (b, b), "W%d2" % b)
        for b in range(4):
            r = "W%d0 W%d1 W%d2 finw" % (b, b, b)
            if b < 3:
                act(T.X[:, b::4], W[b][:].indirect(T.finw[:]), F.Copy, r, "X%d" % b)
            else:
                cp(T.X[:, b::4], W[b][:].indirect(T.finw[:]), r, "X%d" % b)

    quant(T.xq3[:], T.xs3[:], T.X[:], XA, "xq")
    mm(T.pY[:, 0:C], T.vq[:], T.vs[:], T.xq3[:], T.xs3[:], "vq xq", "pY")
    dma("Y", "oc", T.oc[:], u8(T.xq3[:]), "xq", "")
    for k in range(4):
        dma("S" if k < 3 else "Y", "s%d" % k, T.osc[4 * k:4 * k + 4, :], T.xs3[32 * k:32 * k + 4, :], "xq", "")
    cp(T.tmp[:], T.pY[:, 0:C], "pY", "tmp")
    dma("Y", "y", T.y[:], T.tmp[:], "tmp", "")
    _emit(g, T, ops)
    g.wait_ge(T.sem.sent, sent[0])
